import numpy as np
import ml_dtypes


def mxq(x, axis, fmt="e4m3"):
    dtype, down = {"e4m3": (ml_dtypes.float8_e4m3fn, 7), "e5m2": (ml_dtypes.float8_e5m2, 14)}[fmt]
    v = np.moveaxis(np.asarray(x, np.float32).astype(ml_dtypes.bfloat16).astype(np.float64), axis, -1)
    blocks = v.reshape(v.shape[:-1] + (-1, 32))
    amax = np.abs(blocks).max(-1, keepdims=True)
    byte = np.maximum(np.where(amax > 0, np.frexp(amax)[1] - 1 + 127, 0) - down, 1)
    scale = np.exp2(byte - 127.0)
    codes = (blocks / scale).astype(np.float32).astype(dtype).astype(np.float64)
    return np.moveaxis((codes * scale).reshape(v.shape), -1, axis)


WIDE = False


def mx_kscale(k):
    if not WIDE:
        return np.ones(k)
    levels = np.array([10, -10, 5, -5, 0])
    if k % 512:
        return np.exp2(np.random.permutation(np.resize(levels, k // 32))).repeat(32)
    a = np.empty((k // 512, 16))
    for p in range(k // 512):
        a[p, :8] = np.random.permutation(np.resize(levels, 8))
        for g in range(8):
            far = levels[np.abs(levels - a[p, g]) >= 10]
            a[p, g + 8] = far[np.random.randint(len(far))]
    return np.exp2(a.ravel()).repeat(32)


def f64(x):
    return np.asarray(x).astype(np.float64)


def striped(idx):
    return np.tile(idx.reshape(-1, 16).T, (8, 1)).astype(np.uint16)


def unstriped(offs):
    return offs[:16].T.reshape(-1).astype(np.int64)


def striped8(idx):
    return np.concatenate([x.reshape(-1, 16).T for x in idx]).astype(np.uint16)


def runs(offs, k):
    lists = np.stack([offs[16 * r : 16 * r + 16].T.reshape(-1) for r in range(8)]).astype(np.int64)
    return lists[np.arange(k) % 512 // 64]


def pack_weight(w):
    k, n = w.shape
    w = f64(np.asarray(w, np.float32).astype(ml_dtypes.bfloat16)).reshape(k // 32, 32, n)
    amax = np.abs(w).max(1)
    byte = np.clip(np.where(amax > 0, np.frexp(amax)[1] - 1 + 127 - 7, 1), 1, 254)
    scaled = (w * np.exp2(127.0 - byte)[:, None, :]).reshape(k, n).astype(np.float32)
    words = np.ascontiguousarray(scaled.reshape(k // 512, 128, 4, n).transpose(0, 1, 3, 2)).astype(ml_dtypes.float8_e4m3fn).view(np.uint8)
    return words, np.ascontiguousarray(byte.astype(np.uint8).reshape(k // 512, 16, n))


def unpack_weight(words, scales):
    g, p, n, _ = words.shape
    vals = np.ascontiguousarray(words).view(ml_dtypes.float8_e4m3fn).astype(np.float64) * np.repeat(np.exp2(scales.astype(np.float64) - 127.0), 8, axis=1)[..., None]
    return vals.transpose(0, 1, 3, 2).reshape(g * 512, n)


E2M1 = np.array([0.0, 0.5, 1.0, 1.5, 2.0, 3.0, 4.0, 6.0, -0.0, -0.5, -1.0, -1.5, -2.0, -3.0, -4.0, -6.0])


def pack_fp4(w):
    k, n = w.shape
    w = f64(np.asarray(w, np.float32).astype(ml_dtypes.bfloat16)).reshape(k // 32, 32, n)
    amax = np.abs(w).max(1)
    mant, ex = np.frexp(amax / 6.0)
    byte = np.clip(np.where(amax > 0, np.where(mant > 0.5, ex, ex - 1) + 127, 1), 1, 254)
    scaled = (w * np.exp2(127.0 - byte)[:, None, :]).reshape(k, n).astype(np.float32)
    c = np.ascontiguousarray(scaled.reshape(k // 512, 128, 4, n).transpose(0, 1, 3, 2)).astype(ml_dtypes.float4_e2m1fn).view(np.uint8) & 0xF
    words = (c[..., 0::2] | (c[..., 1::2] << 4)).reshape(k // 512, 128, 2 * n)
    return np.ascontiguousarray(words), np.ascontiguousarray(byte.astype(np.uint8).reshape(k // 512, 16, n))


def unpack_fp4(words, scales):
    g, _, n = scales.shape
    words = np.ascontiguousarray(words).reshape(g, 128, n, 2)
    nib = np.empty((g, 128, n, 4), np.uint8)
    nib[..., 0::2] = words & 0xF
    nib[..., 1::2] = words >> 4
    vals = E2M1[nib] * np.repeat(np.exp2(scales.astype(np.float64) - 127.0), 8, axis=1)[..., None]
    return vals.transpose(0, 1, 3, 2).reshape(g * 512, n)


def sigmoid(v):
    return 1.0 / (1.0 + np.exp(-np.maximum(v, -700.0)))

def planes(y):
    n, m = y.shape
    v = y.astype(np.float32).astype(ml_dtypes.bfloat16).astype(np.float64).reshape(n // 32, 32, m)
    top = np.abs(v).max(1)
    byte = np.clip(np.where(top > 0, np.frexp(top)[1] - 1 + 127 - 7, 1), 1, 254)
    codes = (v * np.exp2(127.0 - byte)[:, None, :]).reshape(n, m).astype(np.float32).astype(ml_dtypes.float8_e4m3fn).view(np.uint8)
    words = codes.reshape(n // 512, 128, 4, m).transpose(0, 1, 3, 2)
    return np.ascontiguousarray(words), np.ascontiguousarray(byte.astype(np.uint8).reshape(n // 512, 16, m))


K, T, S, N, G, H = 512, 1024, 512, 512, 2048, 512


def setup_inputs():
    n = np.random.standard_normal
    s = mx_kscale(K)[:, None]
    u = mx_kscale(S)
    packed_xT = pack_weight(n((K, T)) * s)
    packed_dT = pack_weight(n((K, G)) / s)
    packed_w1 = pack_fp4(n((H, N)) / np.sqrt(2 * H) / u[:, None])
    packed_w2 = pack_fp4(n((H, N)) / np.sqrt(2 * H) / u[:, None])
    return {
        "x_words": packed_xT[0],
        "x_scales": packed_xT[1],
        "d_words": packed_dT[0],
        "d_scales": packed_dT[1],
        "gn": (np.random.uniform(0.5, 1.5, (H, 1)) * u[:, None]).astype(np.float32),
        "gm": (np.random.uniform(0.5, 1.5, (H, 1)) * u[:, None]).astype(np.float32),
        "w1_words": packed_w1[0],
        "w1_scales": packed_w1[1],
        "w2_words": packed_w2[0],
        "w2_scales": packed_w2[1],
        "sl": np.random.uniform(1.0, 2.0, (N, 1)).astype(np.float32),
        "th": (0.5 * n((N, 1))).astype(np.float32),
        "offs": striped(np.random.permutation(T)[:S]),
        "k1": striped8(np.random.randint(0, G, (8, H))),
        "two": striped(np.random.permutation(T)[:S]),
        "k2": striped8(np.random.randint(0, G, (8, H))),
        "n1": striped(np.random.randint(0, S, G)),
        "n2": striped8(np.stack([np.random.permutation(S) for _ in range(8)])),
        "n3": striped8(np.stack([np.random.permutation(S) for _ in range(8)])),
        "n4": striped8(np.stack([np.random.permutation(S) for _ in range(8)])),
        "n5": striped8(np.stack([np.random.permutation(S) for _ in range(8)])),
    }


def reference(x_words, x_scales, d_words, d_scales, gn, gm, w1_words, w1_scales, w2_words, w2_scales, sl, th, offs, k1, two, k2, n1, n2, n3, n4, n5):
    d_k1 = unpack_weight(d_words, d_scales)[np.arange(K)[:, None], runs(k1, K)]
    xq = unpack_weight(x_words, x_scales)[:, unstriped(offs)]
    a = 0.0625 * (d_k1.T @ xq)
    mb = a[:, unstriped(n1)]
    mn = mb.reshape(H, S, 4).min(axis=2)
    mx = mb.reshape(H, S, 4).max(axis=2)
    z = f64(gn) * (np.maximum(a, mn) - (0.5 * mx))
    d_k2 = unpack_weight(d_words, d_scales)[np.arange(K)[:, None], runs(k2, K)]
    x_two = unpack_weight(x_words, x_scales)[:, unstriped(two)]
    b = 0.0625 * (d_k2.T @ x_two)
    st = b - (b[np.arange(H)[:, None], runs(n2, H)])
    z2 = f64(gm) * (np.maximum(st, st[np.arange(H)[:, None], runs(n3, H)]))
    h = unpack_fp4(w1_words, w1_scales).T @ mxq(z, 0, "e4m3") + unpack_fp4(w2_words, w2_scales).T @ mxq(z2, 0, "e4m3")
    st2 = h - (h[np.arange(N)[:, None], runs(n4, N)])
    sg = sigmoid(f64(sl) * (st2[np.arange(N)[:, None], runs(n5, N)] - f64(th)))
    out_0 = h * sg
    return (out_0,) + planes(out_0)

@@ -1,0 +1,298 @@
+from contextlib import ExitStack
+
+import concourse.mybir as mybir
+
+F32 = mybir.dt.float32
+BF16 = mybir.dt.bfloat16
+U32 = mybir.dt.uint32
+I32 = mybir.dt.int32
+U16 = mybir.dt.uint16
+U8 = mybir.dt.uint8
+FP8X4 = mybir.dt.float8_e4m3fn_x4
+FP4X4 = mybir.dt.float4_e2m1fn_x4
+ALU = mybir.AluOpType
+ACT = mybir.ActivationFunctionType
+
+P = 128
+T = 4
+S = 512
+TOK = 1024
+G = 2048
+CH = 128
+NCH = S // CH
+HALF = S // 2
+A_WIN = S + 32
+FLOPS = 4 * 2 * 512 * 512 * 512
+
+
+def tile_picked_pqjgmidhopmxehq_none_po_kernel(
+    tc, x_words, x_scales, d_words, d_scales, gn, gm, w1_words, w1_scales, w2_words, w2_scales,
+    sl, th, offs, k1, two, k2, n1, n2, n3, n4, n5, out_0, out_1, out_2,
+):
+    nc = tc.nc
+    with ExitStack() as ctx:
+        lists = ctx.enter_context(tc.tile_pool(name="lists", bufs=1))
+        sb = ctx.enter_context(tc.tile_pool(name="sb", bufs=1))
+        psum = ctx.enter_context(tc.psum_pool(name="psum", bufs=1))
+
+        def tile(name, shape, dtype, tag=None):
+            return sb.tile(shape, dtype, name=name, tag=tag or name, align_bytes=64)
+
+        def load_list(name, src):
+            t = lists.tile([P, src.shape[1]], U16, name=name)
+            nc.sync.dma_start(t[:], src)
+            return t
+
+        d_sc = tile("d_sc", [P, G], U8)
+        x_sc = tile("x_sc", [P, TOK], U8)
+        nc.gpsimd.memset(d_sc[:].bitcast(I32), 0)
+        nc.vector.memset(x_sc[:].bitcast(I32), 0)
+        nc.scalar.dma_start(out=d_sc[0:P:8, :].bitcast(I32), in_=d_scales[0].bitcast(I32))
+        nc.scalar.dma_start(out=x_sc[0:P:8, :].bitcast(I32), in_=x_scales[0].bitcast(I32))
+        l_k1 = load_list("l_k1", k1)
+        l_offs = load_list("l_offs", offs)
+        l_k2 = load_list("l_k2", k2)
+        l_two = load_list("l_two", two)
+        l_n1 = load_list("l_n1", n1)
+        d_w = tile("d_w", [P, G], U32)
+        x_w = tile("x_w", [P, TOK], U32)
+        nc.sync.dma_start(out=d_w[:].bitcast(I32), in_=d_words[0].rearrange("p n t -> p (n t)").bitcast(I32))
+        nc.sync.dma_start(out=x_w[:].bitcast(I32), in_=x_words[0].rearrange("p n t -> p (n t)").bitcast(I32))
+        l_n2 = load_list("l_n2", n2)
+        l_n3 = load_list("l_n3", n3)
+        l_n4 = load_list("l_n4", n4)
+        l_n5 = load_list("l_n5", n5)
+        w_raw = [tile(f"w_raw{i}", [P, 2 * S], U8) for i in range(2)]
+        for i, src in enumerate((w1_words, w2_words)):
+            nc.sync.dma_start(out=w_raw[i][:].bitcast(I32), in_=src[0].bitcast(I32))
+
+        planes = [tile(f"planes{i}", [P, 2 * S], U8) for i in range(2)]
+        for pl in planes:
+            nc.gpsimd.memset(pl[:].bitcast(I32), 0)
+        a_win = [tile(f"a_win{t}", [P, A_WIN], F32) for t in range(T)]
+        for t in range(T):
+            nc.gpsimd.memset(a_win[t][:, S:], 0.0)
+
+        banks = [psum.tile([P, S], F32, name=f"bank{i}") for i in range(8)]
+
+        def coded_product(i, l_code, l_tok, queue, out_banks):
+            got_sc = tile(f"got_sc{i}", [P, 2 * S], U8)
+            nc.vector.tensor_copy(got_sc[:, :S], d_sc[:].indirect(l_code[:]))
+            nc.vector.tensor_copy(got_sc[:, S:], x_sc[:].indirect(l_tok[:]))
+            for q in range(4):
+                queue.dma_start(
+                    out=planes[i][32 * q : 32 * q + 4, :].bitcast(I32),
+                    in_=got_sc[32 * q : 32 * q + 32 : 8, :].bitcast(I32),
+                )
+            got_d = tile(f"got_d{i}", [P, S], U32)
+            nc.vector.tensor_copy(got_d[:], d_w[:].indirect(l_code[:]))
+            dealt_d = tile(f"dealt_d{i}", [P, S], U32)
+            nc.vector.tensor_copy(
+                dealt_d[:].rearrange("p (t c i) -> p c t i", t=T, i=4),
+                got_d[:].rearrange("p (c i t) -> p c t i", t=T, i=4),
+            )
+            got_x = tile(f"got_x{i}", [P, S], U32)
+            nc.vector.tensor_copy(got_x[:], x_w[:].indirect(l_tok[:]))
+            dealt_sc = tile(f"dealt_sc{i}", [P, S], U8)
+            nc.vector.tensor_copy(
+                dealt_sc[:].rearrange("p (t m) -> p t m", t=T),
+                planes[i][:, :S].rearrange("p (m t) -> p t m", t=T),
+            )
+            for t in range(T):
+                nc.tensor.matmul_mx(
+                    out=out_banks[t][:],
+                    lhsT=dealt_d[:, t * P : (t + 1) * P].bitcast(FP8X4),
+                    lhsT_scale=dealt_sc[:, t * P : (t + 1) * P],
+                    rhs=got_x[:].bitcast(FP8X4),
+                    rhs_scale=planes[i][:, S:],
+                    start=True,
+                    stop=True,
+                )
+
+        coded_product(0, l_k1, l_offs, nc.scalar, banks[0:4])
+        rows = tile("rows", [P, 4, 8], F32, tag="got_d0")
+        for i, src in enumerate((gn, gm, sl, th)):
+            nc.sync.dma_start(out=rows[:, i, :T], in_=src.rearrange("(p t) o -> p (t o)", t=T))
+        g_n, g_m, slope, thr = [rows[:, i, :T] for i in range(4)]
+        coded_product(1, l_k2, l_two, nc.sync, banks[4:8])
+        w_sc_raw = tile("w_sc_raw", [P, 2 * S], U8, tag="got_sc0")
+        nc.gpsimd.memset(w_sc_raw[:].bitcast(I32), 0)
+        for i, src in enumerate((w1_scales, w2_scales)):
+            for q in range(4):
+                nc.sync.dma_start(
+                    out=w_sc_raw[32 * q : 32 * q + 4, i * S : (i + 1) * S].bitcast(I32),
+                    in_=src[0, 4 * q : 4 * q + 4, :].bitcast(I32),
+                )
+
+        w_dealt = [tile(f"w_dealt{i}", [P, 2 * S], U8) for i in range(2)]
+        for i in range(2):
+            nc.scalar.copy(
+                w_dealt[i][:].bitcast(U16).rearrange("p (t m) -> p t m", t=T),
+                w_raw[i][:].bitcast(U16).rearrange("p (m t) -> p t m", t=T),
+            )
+        w_sc = tile("w_sc", [P, 2 * S], U8)
+        nc.vector.tensor_copy(
+            w_sc[:].rearrange("p (i t m) -> p i t m", i=2, t=T),
+            w_sc_raw[:].rearrange("p (i m t) -> p i t m", i=2, t=T),
+        )
+        bias = tile("bias", [P, T], F32)
+        nc.vector.scalar_tensor_tensor(bias[:], slope, -1.0, thr, ALU.mult, ALU.mult)
+
+        def scale_round(dst, src, gain, width):
+            nc.vector.tensor_tensor(
+                dst.rearrange("p (c i t) -> p c t i", t=T, i=4),
+                src.rearrange("p t (c i) -> p c t i", i=4),
+                gain.unsqueeze(1).unsqueeze(3).to_broadcast([P, width // 4, T, 4]),
+                ALU.mult,
+            )
+
+        z_codes = tile("z_codes", [P, S], U32)
+        z_sc = tile("z_sc", [P, S], U8)
+        z2_codes = tile("z2_codes", [P, S], U32)
+        z2_sc = tile("z2_sc", [P, S], U8)
+
+        members = [tile(f"members{c}", [P, T, 4 * CH], F32) for c in range(NCH)]
+        for c in range(NCH):
+            for t in range(T):
+                if c == 0:
+                    nc.scalar.activation(a_win[t][:, :S], banks[t][:], ACT.Copy, scale=0.0625)
+                nc.scalar.activation(
+                    members[c][:, t, :], a_win[t][:].indirect(l_n1[:, c * 32 : (c + 1) * 32]), ACT.Copy
+                )
+
+        b_win = [tile(f"b_win{t}", [P, S], F32) for t in range(T)]
+        st_win = [tile(f"st_win{t}", [P, S], F32) for t in range(T)]
+        b_at = [tile(f"b_at{t}", [P, S], F32) for t in range(T)]
+        for t in range(T):
+            nc.scalar.activation(b_win[t][:], banks[4 + t][:], ACT.Copy, scale=0.0625)
+            for u in range(2):
+                nc.scalar.activation(
+                    b_at[t][:, u * HALF : (u + 1) * HALF],
+                    b_win[t][:].indirect(l_n2[:, u * 16 : (u + 1) * 16]),
+                    ACT.Copy,
+                )
+
+        def step(t):
+            nc.vector.tensor_tensor(st_win[t][:], b_win[t][:], b_at[t][:], ALU.subtract)
+
+        def pairs(c):
+            m = members[c][:].rearrange("p t (j u e) -> p (t j) u e", u=2, e=2)
+            lo = tile(f"lo{c % 2}", [P, T * CH, 2], F32)
+            hi = tile(f"hi{c % 2}", [P, T * CH, 2], F32)
+            nc.vector.tensor_tensor(lo[:], m[:, :, 0, :], m[:, :, 1, :], ALU.min)
+            nc.vector.tensor_tensor(hi[:], m[:, :, 0, :], m[:, :, 1, :], ALU.max)
+            return lo, hi
+
+        def finish_z(c, lo, hi):
+            cols = slice(c * CH, (c + 1) * CH)
+            mn = tile(f"mn{c % 2}", [P, T * CH], F32)
+            mx = tile(f"mx{c % 2}", [P, T * CH], F32)
+            nc.vector.tensor_tensor(mn[:], lo[:, :, 0], lo[:, :, 1], ALU.min)
+            nc.vector.tensor_tensor(mx[:], hi[:, :, 0], hi[:, :, 1], ALU.max)
+            v = tile(f"v{c % 2}", [P, T * CH], F32)
+            for t in range(T):
+                nc.vector.tensor_tensor(
+                    v[:, t * CH : (t + 1) * CH], mn[:, t * CH : (t + 1) * CH], a_win[t][:, cols], ALU.max
+                )
+            y = tile(f"y{c % 2}", [P, T, CH], F32)
+            nc.vector.scalar_tensor_tensor(
+                y[:].rearrange("p t j -> p (t j)"), mx[:], -0.5, v[:], ALU.mult, ALU.add
+            )
+            z16 = tile(f"z16_{c}", [P, T * CH], BF16)
+            scale_round(z16[:], y[:], g_n, CH)
+            nc.vector.quantize_mx(out=z_codes[:, cols].bitcast(FP8X4), scales=z_sc[:, cols], in_=z16[:])
+
+        for c in range(NCH):
+            lo, hi = pairs(c)
+            if c == NCH - 1:
+                step(0)
+                step(1)
+            finish_z(c, lo, hi)
+        step(2)
+        step(3)
+
+        st_at = [tile(f"st_at{u}", [P, T, HALF], F32) for u in range(2)]
+        for u in range(2):
+            for t in range(T):
+                nc.scalar.activation(
+                    st_at[u][:, t, :], st_win[t][:].indirect(l_n3[:, u * 16 : (u + 1) * 16]), ACT.Copy
+                )
+        h_win = [tile(f"h_win{t}", [P, S], F32) for t in range(T)]
+        for u in range(2):
+            cols = slice(u * HALF, (u + 1) * HALF)
+            top = tile(f"top{u}", [P, T, HALF], F32)
+            for t in range(T):
+                nc.vector.tensor_tensor(top[:, t, :], st_win[t][:, cols], st_at[u][:, t, :], ALU.max)
+            z16 = tile(f"z2_16_{u}", [P, T * HALF], BF16)
+            scale_round(z16[:], top[:], g_m, HALF)
+            nc.vector.quantize_mx(out=z2_codes[:, cols].bitcast(FP8X4), scales=z2_sc[:, cols], in_=z16[:])
+            for t in range(T):
+                for i, (codes, scales) in enumerate(((z_codes, z_sc), (z2_codes, z2_sc))):
+                    nc.tensor.matmul_mx(
+                        out=banks[t][:, cols],
+                        lhsT=w_dealt[i][:, 2 * t * P : 2 * (t + 1) * P].bitcast(FP4X4),
+                        lhsT_scale=w_sc[:, i * S + t * P : i * S + (t + 1) * P],
+                        rhs=codes[:, cols].bitcast(FP8X4),
+                        rhs_scale=scales[:, cols],
+                        start=(i == 0),
+                        stop=(i == 1),
+                    )
+            for t in range(T):
+                nc.scalar.copy(h_win[t][:, cols], banks[t][:, cols])
+
+        h_at = [tile(f"h_at{t}", [P, S], F32) for t in range(T)]
+        st2_win = [tile(f"st2_win{t}", [P, S], F32) for t in range(T)]
+        for t in range(T):
+            for u in range(2):
+                dst = h_at[t][:, u * HALF : (u + 1) * HALF]
+                src = h_win[t][:].indirect(l_n4[:, u * 16 : (u + 1) * 16])
+                if t % 2 == 0:
+                    nc.scalar.activation(dst, src, ACT.Copy)
+                else:
+                    nc.vector.tensor_copy(dst, src)
+            if t % 2 == 1:
+                for s in (t - 1, t):
+                    nc.vector.tensor_tensor(st2_win[s][:], h_win[s][:], h_at[s][:], ALU.subtract)
+
+        gate = [tile(f"gate{t}", [P, S], F32) for t in range(T)]
+        res = [tile(f"res{u}", [P, T, HALF], F32) for u in range(2)]
+        out_rows = out_0.rearrange("(p t) j -> p t j", t=T)
+
+        def gated(t, u):
+            cols = slice(u * HALF, (u + 1) * HALF)
+            nc.scalar.activation(
+                gate[t][:, cols],
+                st2_win[t][:].indirect(l_n5[:, u * 16 : (u + 1) * 16]),
+                ACT.Sigmoid,
+                bias=bias[:, t : t + 1],
+                scale=slope[:, t : t + 1],
+            )
+            nc.vector.tensor_tensor(res[u][:, t, :], h_win[t][:, cols], gate[t][:, cols], ALU.mult)
+
+        def hand_out(u):
+            cols = slice(u * HALF, (u + 1) * HALF)
+            nc.sync.dma_start(out=out_rows[:, :, cols], in_=res[u][:])
+            r16 = tile(f"r16_{u}", [P, T * HALF], BF16)
+            nc.vector.tensor_copy(
+                r16[:].rearrange("p (c i t) -> p c t i", t=T, i=4),
+                res[u][:].rearrange("p t (c i) -> p c t i", i=4),
+            )
+            codes = tile(f"o_codes{u}", [P, HALF], U32)
+            scales = tile(f"o_sc{u}", [P, HALF], U8)
+            nc.vector.quantize_mx(out=codes[:].bitcast(FP8X4), scales=scales[:], in_=r16[:])
+            nc.sync.dma_start(
+                out=out_1[0].rearrange("p n t -> p (n t)").bitcast(I32)[:, cols], in_=codes[:].bitcast(I32)
+            )
+            for q in range(4):
+                nc.scalar.dma_start(
+                    out=out_2[0, 4 * q : 4 * q + 4, cols].bitcast(I32),
+                    in_=scales[32 * q : 32 * q + 4, :].bitcast(I32),
+                )
+
+        for t in (0, 1):
+            for u in range(2):
+                gated(t, u)
+        for u in range(2):
+            for t in (2, 3):
+                gated(t, u)
+            hand_out(u)

@@ -18,8 +18,9 @@ T = 4
 S = 512
 TOK = 1024
 G = 2048
-CH = 128
-NCH = S // CH
+PIECE = 128
+CHUNKS = ((0, 128), (128, 128), (256, 128), (384, 128))
+NCH = len(CHUNKS)
 HALF = S // 2
 A_WIN = S + 32
 FLOPS = 4 * 2 * 512 * 512 * 512
@@ -76,7 +77,7 @@ def tile_picked_pqjgmidhopmxehq_none_po_kernel(
         banks = [psum.tile([P, S], F32, name=f"bank{i}") for i in range(8)]
 
         def coded_product(i, l_code, l_tok, queue, out_banks):
-            got_sc = tile(f"got_sc{i}", [P, 2 * S], U8)
+            got_sc = tile(f"got_sc{i}", [P, 2 * S], U8, tag="got_sc0")
             nc.vector.tensor_copy(got_sc[:, :S], d_sc[:].indirect(l_code[:]))
             nc.vector.tensor_copy(got_sc[:, S:], x_sc[:].indirect(l_tok[:]))
             for q in range(4):
@@ -84,14 +85,14 @@ def tile_picked_pqjgmidhopmxehq_none_po_kernel(
                     out=planes[i][32 * q : 32 * q + 4, :].bitcast(I32),
                     in_=got_sc[32 * q : 32 * q + 32 : 8, :].bitcast(I32),
                 )
-            got_d = tile(f"got_d{i}", [P, S], U32)
+            got_d = tile(f"got_d{i}", [P, S], U32, tag=("got_d0", "got_x0")[i])
             nc.vector.tensor_copy(got_d[:], d_w[:].indirect(l_code[:]))
             dealt_d = tile(f"dealt_d{i}", [P, S], U32)
             nc.vector.tensor_copy(
                 dealt_d[:].rearrange("p (t c i) -> p c t i", t=T, i=4),
                 got_d[:].rearrange("p (c i t) -> p c t i", t=T, i=4),
             )
-            got_x = tile(f"got_x{i}", [P, S], U32)
+            got_x = tile(f"got_x{i}", [P, S], U32, tag=("got_x0", "dealt_d0")[i])
             nc.vector.tensor_copy(got_x[:], x_w[:].indirect(l_tok[:]))
             dealt_sc = tile(f"dealt_sc{i}", [P, S], U8)
             nc.vector.tensor_copy(
@@ -109,13 +110,13 @@ def tile_picked_pqjgmidhopmxehq_none_po_kernel(
                     stop=True,
                 )
 
-        coded_product(0, l_k1, l_offs, nc.scalar, banks[0:4])
+        coded_product(0, l_k1, l_offs, nc.sync, banks[0:4])
         rows = tile("rows", [P, 4, 8], F32, tag="got_d0")
         for i, src in enumerate((gn, gm, sl, th)):
             nc.sync.dma_start(out=rows[:, i, :T], in_=src.rearrange("(p t) o -> p (t o)", t=T))
         g_n, g_m, slope, thr = [rows[:, i, :T] for i in range(4)]
         coded_product(1, l_k2, l_two, nc.sync, banks[4:8])
-        w_sc_raw = tile("w_sc_raw", [P, 2 * S], U8, tag="got_sc0")
+        w_sc_raw = tile("w_sc_raw", [P, 2 * S], U8, tag="dealt_sc0")
         nc.gpsimd.memset(w_sc_raw[:].bitcast(I32), 0)
         for i, src in enumerate((w1_scales, w2_scales)):
             for q in range(4):
@@ -151,14 +152,18 @@ def tile_picked_pqjgmidhopmxehq_none_po_kernel(
         z2_codes = tile("z2_codes", [P, S], U32)
         z2_sc = tile("z2_sc", [P, S], U8)
 
-        members = [tile(f"members{c}", [P, T, 4 * CH], F32) for c in range(NCH)]
-        for c in range(NCH):
+        members = [tile(f"members{c}", [P, T, 4 * w], F32) for c, (j0, w) in enumerate(CHUNKS)]
+        for c, (j0, w) in enumerate(CHUNKS):
             for t in range(T):
                 if c == 0:
                     nc.scalar.activation(a_win[t][:, :S], banks[t][:], ACT.Copy, scale=0.0625)
-                nc.scalar.activation(
-                    members[c][:, t, :], a_win[t][:].indirect(l_n1[:, c * 32 : (c + 1) * 32]), ACT.Copy
-                )
+                for k in range(w // PIECE):
+                    col = (j0 + k * PIECE) // 4
+                    nc.scalar.activation(
+                        members[c][:, t, k * 4 * PIECE : (k + 1) * 4 * PIECE],
+                        a_win[t][:].indirect(l_n1[:, col : col + PIECE // 4]),
+                        ACT.Copy,
+                    )
 
         b_win = [tile(f"b_win{t}", [P, S], F32) for t in range(T)]
         st_win = [tile(f"st_win{t}", [P, S], F32) for t in range(T)]
@@ -175,124 +180,164 @@ def tile_picked_pqjgmidhopmxehq_none_po_kernel(
         def step(t):
             nc.vector.tensor_tensor(st_win[t][:], b_win[t][:], b_at[t][:], ALU.subtract)
 
-        def pairs(c):
-            m = members[c][:].rearrange("p t (j u e) -> p (t j) u e", u=2, e=2)
-            lo = tile(f"lo{c % 2}", [P, T * CH, 2], F32)
-            hi = tile(f"hi{c % 2}", [P, T * CH, 2], F32)
-            nc.vector.tensor_tensor(lo[:], m[:, :, 0, :], m[:, :, 1, :], ALU.min)
-            nc.vector.tensor_tensor(hi[:], m[:, :, 0, :], m[:, :, 1, :], ALU.max)
-            return lo, hi
+        def per_chunk(name, tail):
+            return [tile(f"{name}{c}", [P, T * w] + tail, F32, tag=f"{name}{c % 2}") for c, (j0, w) in enumerate(CHUNKS)]
 
-        def finish_z(c, lo, hi):
-            cols = slice(c * CH, (c + 1) * CH)
-            mn = tile(f"mn{c % 2}", [P, T * CH], F32)
-            mx = tile(f"mx{c % 2}", [P, T * CH], F32)
-            nc.vector.tensor_tensor(mn[:], lo[:, :, 0], lo[:, :, 1], ALU.min)
-            nc.vector.tensor_tensor(mx[:], hi[:, :, 0], hi[:, :, 1], ALU.max)
-            v = tile(f"v{c % 2}", [P, T * CH], F32)
+        lo = per_chunk("lo", [2])
+        hi = per_chunk("hi", [2])
+        mn = per_chunk("mn", [])
+        mx = per_chunk("mx", [])
+        v = per_chunk("v", [])
+        y = per_chunk("y", [])
+        z16 = [tile(f"z16_{u}", [P, T * HALF], BF16) for u in range(2)]
+
+        def pair_up(dst, op, c, half):
+            w = CHUNKS[c][1]
+            part = slice(half * 2 * w, (half + 1) * 2 * w)
+            m = members[c][:].rearrange("p t (j u e) -> p (t j) u e", u=2, e=2)
+            nc.vector.tensor_tensor(dst[c][:, part, :], m[:, part, 0, :], m[:, part, 1, :], op)
+
+        def extremes(c):
+            j0, w = CHUNKS[c]
+            nc.vector.tensor_tensor(mn[c][:], lo[c][:, :, 0], lo[c][:, :, 1], ALU.min)
+            nc.vector.tensor_tensor(mx[c][:], hi[c][:, :, 0], hi[c][:, :, 1], ALU.max)
             for t in range(T):
-                nc.vector.tensor_tensor(
-                    v[:, t * CH : (t + 1) * CH], mn[:, t * CH : (t + 1) * CH], a_win[t][:, cols], ALU.max
-                )
-            y = tile(f"y{c % 2}", [P, T, CH], F32)
-            nc.vector.scalar_tensor_tensor(
-                y[:].rearrange("p t j -> p (t j)"), mx[:], -0.5, v[:], ALU.mult, ALU.add
-            )
-            z16 = tile(f"z16_{c}", [P, T * CH], BF16)
-            scale_round(z16[:], y[:], g_n, CH)
-            nc.vector.quantize_mx(out=z_codes[:, cols].bitcast(FP8X4), scales=z_sc[:, cols], in_=z16[:])
+                rows_t = slice(t * w, (t + 1) * w)
+                nc.vector.tensor_tensor(v[c][:, rows_t], mn[c][:, rows_t], a_win[t][:, j0 : j0 + w], ALU.max)
+
+        def mix(c):
+            nc.vector.scalar_tensor_tensor(y[c][:], mx[c][:], -0.5, v[c][:], ALU.mult, ALU.add)
+
+        def round_z(c):
+            j0, w = CHUNKS[c]
+            at = T * (j0 % HALF)
+            scale_round(z16[j0 // HALF][:, at : at + T * w], y[c][:].rearrange("p (t j) -> p t j", t=T), g_n, w)
+
+        def quantise_z(u):
+            cols = slice(u * HALF, (u + 1) * HALF)
+            nc.vector.quantize_mx(out=z_codes[:, cols].bitcast(FP8X4), scales=z_sc[:, cols], in_=z16[u][:])
 
         for c in range(NCH):
-            lo, hi = pairs(c)
+            pair_up(lo, ALU.min, c, 0)
+            if c > 0:
+                mix(c - 1)
+            pair_up(hi, ALU.max, c, 0)
+            if c > 0:
+                round_z(c - 1)
+            pair_up(lo, ALU.min, c, 1)
+            if c == 2:
+                quantise_z(0)
+            pair_up(hi, ALU.max, c, 1)
             if c == NCH - 1:
                 step(0)
-                step(1)
-            finish_z(c, lo, hi)
+            extremes(c)
+        step(1)
+        mix(NCH - 1)
         step(2)
+        round_z(NCH - 1)
         step(3)
+        quantise_z(1)
 
-        st_at = [tile(f"st_at{u}", [P, T, HALF], F32) for u in range(2)]
-        for u in range(2):
-            for t in range(T):
+        h_win = [tile(f"h_win{t}", [P, 2 * S], F32) for t in range(T)]
+        for pair in range(2):
+            for u, t in ((0, 2 * pair), (0, 2 * pair + 1), (1, 2 * pair), (1, 2 * pair + 1)):
                 nc.scalar.activation(
-                    st_at[u][:, t, :], st_win[t][:].indirect(l_n3[:, u * 16 : (u + 1) * 16]), ACT.Copy
+                    h_win[t][:, S + u * HALF : S + (u + 1) * HALF],
+                    st_win[t][:].indirect(l_n3[:, u * 16 : (u + 1) * 16]),
+                    ACT.Copy,
                 )
-        h_win = [tile(f"h_win{t}", [P, S], F32) for t in range(T)]
-        for u in range(2):
-            cols = slice(u * HALF, (u + 1) * HALF)
-            top = tile(f"top{u}", [P, T, HALF], F32)
-            for t in range(T):
-                nc.vector.tensor_tensor(top[:, t, :], st_win[t][:, cols], st_at[u][:, t, :], ALU.max)
-            z16 = tile(f"z2_16_{u}", [P, T * HALF], BF16)
-            scale_round(z16[:], top[:], g_m, HALF)
-            nc.vector.quantize_mx(out=z2_codes[:, cols].bitcast(FP8X4), scales=z2_sc[:, cols], in_=z16[:])
-            for t in range(T):
-                for i, (codes, scales) in enumerate(((z_codes, z_sc), (z2_codes, z2_sc))):
-                    nc.tensor.matmul_mx(
-                        out=banks[t][:, cols],
-                        lhsT=w_dealt[i][:, 2 * t * P : 2 * (t + 1) * P].bitcast(FP4X4),
-                        lhsT_scale=w_sc[:, i * S + t * P : i * S + (t + 1) * P],
-                        rhs=codes[:, cols].bitcast(FP8X4),
-                        rhs_scale=scales[:, cols],
-                        start=(i == 0),
-                        stop=(i == 1),
-                    )
-            for t in range(T):
-                nc.scalar.copy(h_win[t][:, cols], banks[t][:, cols])
+        top = [tile(f"top{u}", [P, T, HALF], F32) for u in range(2)]
+        z2_16 = [tile(f"z2_16_{u}", [P, T * HALF], BF16) for u in range(2)]
 
-        h_at = [tile(f"h_at{t}", [P, S], F32) for t in range(T)]
-        st2_win = [tile(f"st2_win{t}", [P, S], F32) for t in range(T)]
+        def larger(t, u):
+            cols = slice(u * HALF, (u + 1) * HALF)
+            nc.vector.tensor_tensor(top[u][:, t, :], st_win[t][:, cols], h_win[t][:, S + u * HALF : S + (u + 1) * HALF], ALU.max)
+
+        def h_pass(i, u):
+            codes, scales = ((z_codes, z_sc), (z2_codes, z2_sc))[i]
+            cols = slice(u * HALF, (u + 1) * HALF)
+            for t in range(T):
+                nc.tensor.matmul_mx(
+                    out=banks[T * u + t][:, :HALF],
+                    lhsT=w_dealt[i][:, 2 * t * P : 2 * (t + 1) * P].bitcast(FP4X4),
+                    lhsT_scale=w_sc[:, i * S + t * P : i * S + (t + 1) * P],
+                    rhs=codes[:, cols].bitcast(FP8X4),
+                    rhs_scale=scales[:, cols],
+                    start=(i == 0),
+                    stop=(i == 1),
+                )
+
+        def quantise_z2(u):
+            cols = slice(u * HALF, (u + 1) * HALF)
+            nc.vector.quantize_mx(out=z2_codes[:, cols].bitcast(FP8X4), scales=z2_sc[:, cols], in_=z2_16[u][:])
+
+        def fetch_h(u, t):
+            nc.scalar.copy(h_win[t][:, u * HALF : (u + 1) * HALF], banks[T * u + t][:, :HALF])
+
+        h_pass(0, 0)
+        h_pass(0, 1)
+        for t, u in ((0, 0), (1, 0), (0, 1), (1, 1), (2, 0), (3, 0), (2, 1)):
+            larger(t, u)
+        scale_round(z2_16[0][:], top[0][:], g_m, HALF)
+        larger(3, 1)
+        quantise_z2(0)
+        h_pass(1, 0)
         for t in range(T):
-            for u in range(2):
-                dst = h_at[t][:, u * HALF : (u + 1) * HALF]
-                src = h_win[t][:].indirect(l_n4[:, u * 16 : (u + 1) * 16])
-                if t % 2 == 0:
-                    nc.scalar.activation(dst, src, ACT.Copy)
-                else:
-                    nc.vector.tensor_copy(dst, src)
-            if t % 2 == 1:
-                for s in (t - 1, t):
-                    nc.vector.tensor_tensor(st2_win[s][:], h_win[s][:], h_at[s][:], ALU.subtract)
+            fetch_h(0, t)
+        scale_round(z2_16[1][:], top[1][:], g_m, HALF)
+        quantise_z2(1)
+        h_pass(1, 1)
+
+        st2_win = [tile(f"st2_win{t}", [P, 2 * S if t < 2 else S], F32) for t in range(T)]
+        h_at_own = [tile(f"h_at{t}", [P, S], F32) for t in (2, 3)]
+        h_at = [st2_win[0][:, S:], st2_win[1][:, S:], h_at_own[0][:], h_at_own[1][:]]
+        for pair in range(2):
+            even, odd = 2 * pair, 2 * pair + 1
+            fetch_h(1, odd)
+            fetch_h(1, even)
+            nc.vector.tensor_copy(h_at[odd], h_win[odd][:].indirect(l_n4[:]))
+            nc.scalar.activation(h_at[even], h_win[even][:].indirect(l_n4[:]), ACT.Copy)
+            for s in (even, odd):
+                nc.vector.tensor_tensor(st2_win[s][:, :S], h_win[s][:, :S], h_at[s], ALU.subtract)
 
         gate = [tile(f"gate{t}", [P, S], F32) for t in range(T)]
-        res = [tile(f"res{u}", [P, T, HALF], F32) for u in range(2)]
+        res = tile("res", [P, T, S], F32)
+        r16 = tile("r16", [P, T * S], BF16)
+        o_codes = tile("o_codes", [P, S], U32)
+        o_sc = tile("o_sc", [P, S], U8)
         out_rows = out_0.rearrange("(p t) j -> p t j", t=T)
+        out_words = out_1[0].rearrange("p n t -> p (n t)").bitcast(I32)
 
-        def gated(t, u):
-            cols = slice(u * HALF, (u + 1) * HALF)
+        def gated(t, j0, w):
+            cols = slice(j0, j0 + w)
             nc.scalar.activation(
                 gate[t][:, cols],
-                st2_win[t][:].indirect(l_n5[:, u * 16 : (u + 1) * 16]),
+                st2_win[t][:].indirect(l_n5[:, j0 // 16 : (j0 + w) // 16]),
                 ACT.Sigmoid,
                 bias=bias[:, t : t + 1],
                 scale=slope[:, t : t + 1],
             )
-            nc.vector.tensor_tensor(res[u][:, t, :], h_win[t][:, cols], gate[t][:, cols], ALU.mult)
+            nc.vector.tensor_tensor(res[:, t, cols], h_win[t][:, cols], gate[t][:, cols], ALU.mult)
 
-        def hand_out(u):
-            cols = slice(u * HALF, (u + 1) * HALF)
-            nc.sync.dma_start(out=out_rows[:, :, cols], in_=res[u][:])
-            r16 = tile(f"r16_{u}", [P, T * HALF], BF16)
+        def hand_out(j0, w):
+            cols = slice(j0, j0 + w)
+            nc.sync.dma_start(out=out_rows[:, 2:4, cols], in_=res[:, 2:4, cols])
+            part = r16[:, T * j0 : T * (j0 + w)]
             nc.vector.tensor_copy(
-                r16[:].rearrange("p (c i t) -> p c t i", t=T, i=4),
-                res[u][:].rearrange("p t (c i) -> p c t i", i=4),
+                part.rearrange("p (c i t) -> p c t i", t=T, i=4),
+                res[:, :, cols].rearrange("p t (c i) -> p c t i", i=4),
             )
-            codes = tile(f"o_codes{u}", [P, HALF], U32)
-            scales = tile(f"o_sc{u}", [P, HALF], U8)
-            nc.vector.quantize_mx(out=codes[:].bitcast(FP8X4), scales=scales[:], in_=r16[:])
-            nc.sync.dma_start(
-                out=out_1[0].rearrange("p n t -> p (n t)").bitcast(I32)[:, cols], in_=codes[:].bitcast(I32)
-            )
-            for q in range(4):
-                nc.scalar.dma_start(
-                    out=out_2[0, 4 * q : 4 * q + 4, cols].bitcast(I32),
-                    in_=scales[32 * q : 32 * q + 4, :].bitcast(I32),
-                )
+            nc.vector.quantize_mx(out=o_codes[:, cols].bitcast(FP8X4), scales=o_sc[:, cols], in_=part)
+            nc.sync.dma_start(out=out_words[:, cols], in_=o_codes[:, cols].bitcast(I32))
 
         for t in (0, 1):
-            for u in range(2):
-                gated(t, u)
-        for u in range(2):
+            gated(t, 0, S)
+        nc.sync.dma_start(out=out_rows[:, 0:2, :], in_=res[:, 0:2, :])
+        for j0, w in ((0, 256), (256, 128), (384, 128)):
             for t in (2, 3):
-                gated(t, u)
-            hand_out(u)
+                gated(t, j0, w)
+            hand_out(j0, w)
+        for q in range(4):
+            nc.scalar.dma_start(
+                out=out_2[0, 4 * q : 4 * q + 4, :].bitcast(I32), in_=o_sc[32 * q : 32 * q + 4, :].bitcast(I32)
+            )

@@ -141,9 +141,9 @@ def tile_picked_pqjgmidhopmxehq_none_po_kernel(
 
         def scale_round(dst, src, gain, width):
             nc.vector.tensor_tensor(
-                dst.rearrange("p (c i t) -> p c t i", t=T, i=4),
-                src.rearrange("p t (c i) -> p c t i", i=4),
-                gain.unsqueeze(1).unsqueeze(3).to_broadcast([P, width // 4, T, 4]),
+                dst.rearrange("p (c i t) -> p c t i", t=T, i=2),
+                src.rearrange("p t (c i) -> p c t i", i=2),
+                gain.unsqueeze(1).unsqueeze(3).to_broadcast([P, width // 2, T, 2]),
                 ALU.mult,
             )
 
@@ -191,9 +191,9 @@ def tile_picked_pqjgmidhopmxehq_none_po_kernel(
         y = per_chunk("y", [])
         z16 = [tile(f"z16_{u}", [P, T * HALF], BF16) for u in range(2)]
 
-        def pair_up(dst, op, c, half):
+        def pair_up(dst, op, c, t0, t1):
             w = CHUNKS[c][1]
-            part = slice(half * 2 * w, (half + 1) * 2 * w)
+            part = slice(t0 * w, t1 * w)
             m = members[c][:].rearrange("p t (j u e) -> p (t j) u e", u=2, e=2)
             nc.vector.tensor_tensor(dst[c][:, part, :], m[:, part, 0, :], m[:, part, 1, :], op)
 
@@ -218,19 +218,21 @@ def tile_picked_pqjgmidhopmxehq_none_po_kernel(
             nc.vector.quantize_mx(out=z_codes[:, cols].bitcast(FP8X4), scales=z_sc[:, cols], in_=z16[u][:])
 
         for c in range(NCH):
-            pair_up(lo, ALU.min, c, 0)
+            split = 2 if c < 2 else T
+            pair_up(lo, ALU.min, c, 0, split)
             if c > 0:
                 mix(c - 1)
-            pair_up(hi, ALU.max, c, 0)
+            pair_up(hi, ALU.max, c, 0, split)
             if c > 0:
                 round_z(c - 1)
-            pair_up(lo, ALU.min, c, 1)
-            if c == 2:
-                quantise_z(0)
-            pair_up(hi, ALU.max, c, 1)
+            if split < T:
+                pair_up(lo, ALU.min, c, split, T)
+                pair_up(hi, ALU.max, c, split, T)
             if c == NCH - 1:
                 step(0)
             extremes(c)
+            if c == 2:
+                quantise_z(0)
         step(1)
         mix(NCH - 1)
         step(2)
@@ -319,24 +321,34 @@ def tile_picked_pqjgmidhopmxehq_none_po_kernel(
             )
             nc.vector.tensor_tensor(res[:, t, cols], h_win[t][:, cols], gate[t][:, cols], ALU.mult)
 
-        def hand_out(j0, w):
+        def round_out(j0, w):
             cols = slice(j0, j0 + w)
             nc.sync.dma_start(out=out_rows[:, 2:4, cols], in_=res[:, 2:4, cols])
-            part = r16[:, T * j0 : T * (j0 + w)]
             nc.vector.tensor_copy(
-                part.rearrange("p (c i t) -> p c t i", t=T, i=4),
-                res[:, :, cols].rearrange("p t (c i) -> p c t i", i=4),
+                r16[:, T * j0 : T * (j0 + w)].rearrange("p (c i t) -> p c t i", t=T, i=2),
+                res[:, :, cols].rearrange("p t (c i) -> p c t i", i=2),
             )
-            nc.vector.quantize_mx(out=o_codes[:, cols].bitcast(FP8X4), scales=o_sc[:, cols], in_=part)
+
+        def quantise_out(j0, w):
+            cols = slice(j0, j0 + w)
+            nc.vector.quantize_mx(
+                out=o_codes[:, cols].bitcast(FP8X4), scales=o_sc[:, cols], in_=r16[:, T * j0 : T * (j0 + w)]
+            )
             nc.sync.dma_start(out=out_words[:, cols], in_=o_codes[:, cols].bitcast(I32))
 
         for t in (0, 1):
             gated(t, 0, S)
         nc.sync.dma_start(out=out_rows[:, 0:2, :], in_=res[:, 0:2, :])
-        for j0, w in ((0, 256), (256, 128), (384, 128)):
-            for t in (2, 3):
-                gated(t, j0, w)
-            hand_out(j0, w)
+        pieces = ((0, 256), (256, 128), (384, 128))
+        gated(2, *pieces[0])
+        gated(3, *pieces[0])
+        for k in range(1, len(pieces)):
+            gated(2, *pieces[k])
+            round_out(*pieces[k - 1])
+            gated(3, *pieces[k])
+            quantise_out(*pieces[k - 1])
+        round_out(*pieces[-1])
+        quantise_out(*pieces[-1])
         for q in range(4):
             nc.scalar.dma_start(
                 out=out_2[0, 4 * q : 4 * q + 4, :].bitcast(I32), in_=o_sc[32 * q : 32 * q + 4, :].bitcast(I32)

@@ -48,6 +48,10 @@ def tile_picked_pqjgmidhopmxehq_none_po_kernel(
         x_sc = tile("x_sc", [P, TOK], U8)
         nc.gpsimd.memset(d_sc[:].bitcast(I32), 0)
         nc.vector.memset(x_sc[:].bitcast(I32), 0)
+        warm_in = tile("warm_in", [P, 1], F32)
+        warm_out = tile("warm_out", [P, 1], F32)
+        nc.gpsimd.memset(warm_in[:], 0.0)
+        nc.scalar.activation(warm_out[:], warm_in[:], ACT.Sigmoid)
         nc.scalar.dma_start(out=d_sc[0:P:8, :].bitcast(I32), in_=d_scales[0].bitcast(I32))
         nc.scalar.dma_start(out=x_sc[0:P:8, :].bitcast(I32), in_=x_scales[0].bitcast(I32))
         l_k1 = load_list("l_k1", k1)

@@ -12,6 +12,7 @@ FP8X4 = mybir.dt.float8_e4m3fn_x4
 FP4X4 = mybir.dt.float4_e2m1fn_x4
 ALU = mybir.AluOpType
 ACT = mybir.ActivationFunctionType
+AX = mybir.AxisListType
 
 P = 128
 T = 4
@@ -78,6 +79,10 @@ def tile_picked_pqjgmidhopmxehq_none_po_kernel(
         for t in range(T):
             nc.gpsimd.memset(a_win[t][:, S:], 0.0)
 
+        b_win = [tile(f"b_win{t}", [P, 2 * S], F32) for t in range(T)]
+        for t in range(T):
+            nc.gpsimd.memset(b_win[t][:, S:], 0.0)
+
         banks = [psum.tile([P, S], F32, name=f"bank{i}") for i in range(8)]
 
         def coded_product(i, l_code, l_tok, queue, out_banks):
@@ -135,13 +140,11 @@ def tile_picked_pqjgmidhopmxehq_none_po_kernel(
                 w_dealt[i][:].bitcast(U16).rearrange("p (t m) -> p t m", t=T),
                 w_raw[i][:].bitcast(U16).rearrange("p (m t) -> p t m", t=T),
             )
-        w_sc = tile("w_sc", [P, 2 * S], U8)
-        nc.vector.tensor_copy(
-            w_sc[:].rearrange("p (i t m) -> p i t m", i=2, t=T),
-            w_sc_raw[:].rearrange("p (i m t) -> p i t m", i=2, t=T),
-        )
         bias = tile("bias", [P, T], F32)
         nc.vector.scalar_tensor_tensor(bias[:], slope, -1.0, thr, ALU.mult, ALU.mult)
+
+        g_n16 = tile("g_n16", [P, T], F32)
+        nc.vector.tensor_scalar(g_n16[:], g_n, 0.0625, None, ALU.mult)
 
         def scale_round(dst, src, gain, width):
             nc.vector.tensor_tensor(
@@ -160,7 +163,7 @@ def tile_picked_pqjgmidhopmxehq_none_po_kernel(
         for c, (j0, w) in enumerate(CHUNKS):
             for t in range(T):
                 if c == 0:
-                    nc.scalar.activation(a_win[t][:, :S], banks[t][:], ACT.Copy, scale=0.0625)
+                    nc.scalar.activation(a_win[t][:, :S], banks[t][:], ACT.Copy, scale=0.5)
                 for k in range(w // PIECE):
                     col = (j0 + k * PIECE) // 4
                     nc.scalar.activation(
@@ -169,78 +172,104 @@ def tile_picked_pqjgmidhopmxehq_none_po_kernel(
                         ACT.Copy,
                     )
 
-        b_win = [tile(f"b_win{t}", [P, S], F32) for t in range(T)]
-        st_win = [tile(f"st_win{t}", [P, S], F32) for t in range(T)]
         b_at = [tile(f"b_at{t}", [P, S], F32) for t in range(T)]
-        for t in range(T):
-            nc.scalar.activation(b_win[t][:], banks[4 + t][:], ACT.Copy, scale=0.0625)
-            for u in range(2):
-                nc.scalar.activation(
-                    b_at[t][:, u * HALF : (u + 1) * HALF],
-                    b_win[t][:].indirect(l_n2[:, u * 16 : (u + 1) * 16]),
-                    ACT.Copy,
-                )
+        nc.scalar.activation(b_win[0][:, :S], banks[T][:], ACT.Copy, scale=0.0625)
 
-        def step(t):
-            nc.vector.tensor_tensor(st_win[t][:], b_win[t][:], b_at[t][:], ALU.subtract)
+        def fetch_b(t):
+            nc.vector.tensor_scalar(b_win[t][:, :S], banks[T + t][:], 0.0625, None, ALU.mult)
 
-        def per_chunk(name, tail):
-            return [tile(f"{name}{c}", [P, T * w] + tail, F32, tag=f"{name}{c % 2}") for c, (j0, w) in enumerate(CHUNKS)]
+        def per_chunk(name):
+            return [tile(f"{name}{c}", [P, T * w], F32, tag=f"{name}{c % 2}") for c, (j0, w) in enumerate(CHUNKS)]
 
-        lo = per_chunk("lo", [2])
-        hi = per_chunk("hi", [2])
-        mn = per_chunk("mn", [])
-        mx = per_chunk("mx", [])
-        v = per_chunk("v", [])
-        y = per_chunk("y", [])
+        mn = per_chunk("mn")
+        mx = per_chunk("mx")
+        v = per_chunk("v")
+        y = per_chunk("y")
         z16 = [tile(f"z16_{u}", [P, T * HALF], BF16) for u in range(2)]
 
-        def pair_up(dst, op, c, t0, t1):
-            w = CHUNKS[c][1]
-            part = slice(t0 * w, t1 * w)
-            m = members[c][:].rearrange("p t (j u e) -> p (t j) u e", u=2, e=2)
-            nc.vector.tensor_tensor(dst[c][:, part, :], m[:, part, 0, :], m[:, part, 1, :], op)
+        hi = [tile(f"hi{c}", [P, T * w, 2], F32, tag="hi") for c, (j0, w) in enumerate(CHUNKS)]
 
-        def extremes(c):
-            j0, w = CHUNKS[c]
-            nc.vector.tensor_tensor(mn[c][:], lo[c][:, :, 0], lo[c][:, :, 1], ALU.min)
+        def smallest(c, t0, t1):
+            w = CHUNKS[c][1]
+            m = members[c][:, t0:t1, :].rearrange("p t (j e) -> p (t j) e", e=4)
+            nc.vector.tensor_reduce(mn[c][:, t0 * w : t1 * w], m, AX.X, ALU.min)
+
+        def larger_of_pairs(c, t0, t1):
+            w = CHUNKS[c][1]
+            m = members[c][:, t0:t1, :].rearrange("p t (j u e) -> p (t j) u e", u=2, e=2)
+            nc.vector.tensor_tensor(hi[c][:, t0 * w : t1 * w, :], m[:, :, 0, :], m[:, :, 1, :], ALU.max)
+
+        def largest(c):
             nc.vector.tensor_tensor(mx[c][:], hi[c][:, :, 0], hi[c][:, :, 1], ALU.max)
+
+        def against_own(c):
+            j0, w = CHUNKS[c]
             for t in range(T):
                 rows_t = slice(t * w, (t + 1) * w)
-                nc.vector.tensor_tensor(v[c][:, rows_t], mn[c][:, rows_t], a_win[t][:, j0 : j0 + w], ALU.max)
+                nc.vector.scalar_tensor_tensor(
+                    v[c][:, rows_t], mn[c][:, rows_t], 2.0, banks[t][:, j0 : j0 + w], ALU.mult, ALU.max
+                )
 
-        def mix(c):
-            nc.vector.scalar_tensor_tensor(y[c][:], mx[c][:], -0.5, v[c][:], ALU.mult, ALU.add)
+        def mix(c, eng):
+            eng.tensor_tensor(y[c][:], v[c][:], mx[c][:], ALU.subtract)
 
-        def round_z(c):
+        def z16_part(c):
             j0, w = CHUNKS[c]
             at = T * (j0 % HALF)
-            scale_round(z16[j0 // HALF][:, at : at + T * w], y[c][:].rearrange("p (t j) -> p t j", t=T), g_n, w)
+            return z16[j0 // HALF][:, at : at + T * w]
+
+        def round_z_aside(c):
+            w = CHUNKS[c][1]
+            nc.gpsimd.tensor_tensor(
+                z16_part(c).rearrange("p (j t) -> p j t", t=T),
+                y[c][:].rearrange("p (t j) -> p j t", t=T),
+                g_n16[:].unsqueeze(1).to_broadcast([P, w, T]),
+                ALU.mult,
+            )
 
         def quantise_z(u):
             cols = slice(u * HALF, (u + 1) * HALF)
             nc.vector.quantize_mx(out=z_codes[:, cols].bitcast(FP8X4), scales=z_sc[:, cols], in_=z16[u][:])
 
+        st_win = [tile(f"st_win{t}", [P, S], F32) for t in range(T)]
+
+        def step(t):
+            nc.scalar.activation(b_at[t][:], b_win[t][:].indirect(l_n2[:]), ACT.Copy)
+            nc.vector.tensor_tensor(st_win[t][:], b_win[t][:, :S], b_at[t][:], ALU.subtract)
+
+        last = NCH - 1
         for c in range(NCH):
-            split = 2 if c < 2 else T
-            pair_up(lo, ALU.min, c, 0, split)
-            if c > 0:
-                mix(c - 1)
-            pair_up(hi, ALU.max, c, 0, split)
-            if c > 0:
-                round_z(c - 1)
-            if split < T:
-                pair_up(lo, ALU.min, c, split, T)
-                pair_up(hi, ALU.max, c, split, T)
-            if c == NCH - 1:
-                step(0)
-            extremes(c)
+            if c in (1, 2):
+                fetch_b(c + 1)
+            smallest(c, 0, 2)
+            if c == 0:
+                larger_of_pairs(c, 0, 2)
+                fetch_b(1)
+            smallest(c, 2, T)
+            if c == 0:
+                larger_of_pairs(c, 2, T)
+                against_own(c)
+            else:
+                against_own(c)
+                larger_of_pairs(c, 0, T)
+            if c == 1:
+                w_sc = tile("w_sc", [P, 2 * S], U8, tag="members0")
+                nc.vector.tensor_copy(
+                    w_sc[:].rearrange("p (i t m) -> p i t m", i=2, t=T),
+                    w_sc_raw[:].rearrange("p (i m t) -> p i t m", i=2, t=T),
+                )
             if c == 2:
                 quantise_z(0)
+            if c == last:
+                step(0)
+            largest(c)
+            if c < last:
+                mix(c, nc.gpsimd)
+                round_z_aside(c)
         step(1)
-        mix(NCH - 1)
+        mix(last, nc.vector)
         step(2)
-        round_z(NCH - 1)
+        scale_round(z16_part(last), y[last][:].rearrange("p (t j) -> p t j", t=T), g_n16[:], CHUNKS[last][1])
         step(3)
         quantise_z(1)
 
@@ -262,7 +291,7 @@ def tile_picked_pqjgmidhopmxehq_none_po_kernel(
         def h_pass(i, u):
             codes, scales = ((z_codes, z_sc), (z2_codes, z2_sc))[i]
             cols = slice(u * HALF, (u + 1) * HALF)
-            for t in range(T):
+            for t in (1, 0, 3, 2):
                 nc.tensor.matmul_mx(
                     out=banks[T * u + t][:, :HALF],
                     lhsT=w_dealt[i][:, 2 * t * P : 2 * (t + 1) * P].bitcast(FP4X4),

from contextlib import ExitStack

import concourse.mybir as mybir

F32 = mybir.dt.float32
BF16 = mybir.dt.bfloat16
U32 = mybir.dt.uint32
I32 = mybir.dt.int32
U16 = mybir.dt.uint16
U8 = mybir.dt.uint8
FP8X4 = mybir.dt.float8_e4m3fn_x4
FP4X4 = mybir.dt.float4_e2m1fn_x4
ALU = mybir.AluOpType
ACT = mybir.ActivationFunctionType
AX = mybir.AxisListType

P = 128
T = 4
S = 512
TOK = 1024
G = 2048
PIECE = 128
CHUNKS = ((0, 128), (128, 128), (256, 128), (384, 128))
NCH = len(CHUNKS)
HALF = S // 2
A_WIN = S + 32
FLOPS = 4 * 2 * 512 * 512 * 512


def tile_picked_pqjgmidhopmxehq_none_po_kernel(
    tc, x_words, x_scales, d_words, d_scales, gn, gm, w1_words, w1_scales, w2_words, w2_scales,
    sl, th, offs, k1, two, k2, n1, n2, n3, n4, n5, out_0, out_1, out_2,
):
    nc = tc.nc
    with ExitStack() as ctx:
        lists = ctx.enter_context(tc.tile_pool(name="lists", bufs=1))
        sb = ctx.enter_context(tc.tile_pool(name="sb", bufs=1))
        psum = ctx.enter_context(tc.psum_pool(name="psum", bufs=1))

        def tile(name, shape, dtype, tag=None):
            return sb.tile(shape, dtype, name=name, tag=tag or name, align_bytes=64)

        def load_list(name, src):
            t = lists.tile([P, src.shape[1]], U16, name=name)
            nc.sync.dma_start(t[:], src)
            return t

        d_sc = tile("d_sc", [P, G], U8)
        x_sc = tile("x_sc", [P, TOK], U8)
        nc.gpsimd.memset(d_sc[:].bitcast(I32), 0)
        nc.vector.memset(x_sc[:].bitcast(I32), 0)
        warm_in = tile("warm_in", [P, 1], F32)
        warm_out = tile("warm_out", [P, 1], F32)
        nc.gpsimd.memset(warm_in[:], 0.0)
        nc.scalar.activation(warm_out[:], warm_in[:], ACT.Sigmoid)
        nc.scalar.dma_start(out=d_sc[0:P:8, :].bitcast(I32), in_=d_scales[0].bitcast(I32))
        nc.scalar.dma_start(out=x_sc[0:P:8, :].bitcast(I32), in_=x_scales[0].bitcast(I32))
        l_k1 = load_list("l_k1", k1)
        l_offs = load_list("l_offs", offs)
        l_k2 = load_list("l_k2", k2)
        l_two = load_list("l_two", two)
        l_n1 = load_list("l_n1", n1)
        d_w = tile("d_w", [P, G], U32)
        x_w = tile("x_w", [P, TOK], U32)
        nc.sync.dma_start(out=d_w[:].bitcast(I32), in_=d_words[0].rearrange("p n t -> p (n t)").bitcast(I32))
        nc.sync.dma_start(out=x_w[:].bitcast(I32), in_=x_words[0].rearrange("p n t -> p (n t)").bitcast(I32))
        l_n2 = load_list("l_n2", n2)
        l_n3 = load_list("l_n3", n3)
        l_n4 = load_list("l_n4", n4)
        l_n5 = load_list("l_n5", n5)
        w_raw = [tile(f"w_raw{i}", [P, 2 * S], U8) for i in range(2)]
        for i, src in enumerate((w1_words, w2_words)):
            nc.sync.dma_start(out=w_raw[i][:].bitcast(I32), in_=src[0].bitcast(I32))

        planes = [tile(f"planes{i}", [P, 2 * S], U8) for i in range(2)]
        for pl in planes:
            nc.gpsimd.memset(pl[:].bitcast(I32), 0)
        a_win = [tile(f"a_win{t}", [P, A_WIN], F32) for t in range(T)]
        for t in range(T):
            nc.gpsimd.memset(a_win[t][:, S:], 0.0)

        b_win = [tile(f"b_win{t}", [P, 2 * S], F32) for t in range(T)]
        for t in range(T):
            nc.gpsimd.memset(b_win[t][:, S:], 0.0)

        banks = [psum.tile([P, S], F32, name=f"bank{i}") for i in range(8)]

        def coded_product(i, l_code, l_tok, queue, out_banks):
            got_sc = tile(f"got_sc{i}", [P, 2 * S], U8, tag="got_sc0")
            nc.vector.tensor_copy(got_sc[:, :S], d_sc[:].indirect(l_code[:]))
            nc.vector.tensor_copy(got_sc[:, S:], x_sc[:].indirect(l_tok[:]))
            for q in range(4):
                queue.dma_start(
                    out=planes[i][32 * q : 32 * q + 4, :].bitcast(I32),
                    in_=got_sc[32 * q : 32 * q + 32 : 8, :].bitcast(I32),
                )
            got_d = tile(f"got_d{i}", [P, S], U32, tag=("got_d0", "got_x0")[i])
            nc.vector.tensor_copy(got_d[:], d_w[:].indirect(l_code[:]))
            dealt_d = tile(f"dealt_d{i}", [P, S], U32)
            nc.vector.tensor_copy(
                dealt_d[:].rearrange("p (t c i) -> p c t i", t=T, i=4),
                got_d[:].rearrange("p (c i t) -> p c t i", t=T, i=4),
            )
            got_x = tile(f"got_x{i}", [P, S], U32, tag=("got_x0", "dealt_d0")[i])
            nc.vector.tensor_copy(got_x[:], x_w[:].indirect(l_tok[:]))
            dealt_sc = tile(f"dealt_sc{i}", [P, S], U8)
            nc.vector.tensor_copy(
                dealt_sc[:].rearrange("p (t m) -> p t m", t=T),
                planes[i][:, :S].rearrange("p (m t) -> p t m", t=T),
            )
            for t in range(T):
                nc.tensor.matmul_mx(
                    out=out_banks[t][:],
                    lhsT=dealt_d[:, t * P : (t + 1) * P].bitcast(FP8X4),
                    lhsT_scale=dealt_sc[:, t * P : (t + 1) * P],
                    rhs=got_x[:].bitcast(FP8X4),
                    rhs_scale=planes[i][:, S:],
                    start=True,
                    stop=True,
                )

        coded_product(0, l_k1, l_offs, nc.sync, banks[0:4])
        rows = tile("rows", [P, 4, 8], F32, tag="got_d0")
        for i, src in enumerate((gn, gm, sl, th)):
            nc.sync.dma_start(out=rows[:, i, :T], in_=src.rearrange("(p t) o -> p (t o)", t=T))
        g_n, g_m, slope, thr = [rows[:, i, :T] for i in range(4)]
        coded_product(1, l_k2, l_two, nc.sync, banks[4:8])
        w_sc_raw = tile("w_sc_raw", [P, 2 * S], U8, tag="dealt_sc0")
        nc.gpsimd.memset(w_sc_raw[:].bitcast(I32), 0)
        for i, src in enumerate((w1_scales, w2_scales)):
            for q in range(4):
                nc.sync.dma_start(
                    out=w_sc_raw[32 * q : 32 * q + 4, i * S : (i + 1) * S].bitcast(I32),
                    in_=src[0, 4 * q : 4 * q + 4, :].bitcast(I32),
                )

        w_dealt = [tile(f"w_dealt{i}", [P, 2 * S], U8) for i in range(2)]
        for i in range(2):
            nc.scalar.copy(
                w_dealt[i][:].bitcast(U16).rearrange("p (t m) -> p t m", t=T),
                w_raw[i][:].bitcast(U16).rearrange("p (m t) -> p t m", t=T),
            )
        bias = tile("bias", [P, T], F32)
        nc.vector.scalar_tensor_tensor(bias[:], slope, -1.0, thr, ALU.mult, ALU.mult)

        g_n16 = tile("g_n16", [P, T], F32)
        nc.vector.tensor_scalar(g_n16[:], g_n, 0.0625, None, ALU.mult)

        def scale_round(dst, src, gain, width):
            nc.vector.tensor_tensor(
                dst.rearrange("p (c i t) -> p c t i", t=T, i=2),
                src.rearrange("p t (c i) -> p c t i", i=2),
                gain.unsqueeze(1).unsqueeze(3).to_broadcast([P, width // 2, T, 2]),
                ALU.mult,
            )

        z_codes = tile("z_codes", [P, S], U32)
        z_sc = tile("z_sc", [P, S], U8)
        z2_codes = tile("z2_codes", [P, S], U32)
        z2_sc = tile("z2_sc", [P, S], U8)

        members = [tile(f"members{c}", [P, T, 4 * w], F32) for c, (j0, w) in enumerate(CHUNKS)]
        for c, (j0, w) in enumerate(CHUNKS):
            for t in range(T):
                if c == 0:
                    nc.scalar.activation(a_win[t][:, :S], banks[t][:], ACT.Copy, scale=0.5)
                for k in range(w // PIECE):
                    col = (j0 + k * PIECE) // 4
                    nc.scalar.activation(
                        members[c][:, t, k * 4 * PIECE : (k + 1) * 4 * PIECE],
                        a_win[t][:].indirect(l_n1[:, col : col + PIECE // 4]),
                        ACT.Copy,
                    )

        b_at = [tile(f"b_at{t}", [P, S], F32) for t in range(T)]
        nc.scalar.activation(b_win[0][:, :S], banks[T][:], ACT.Copy, scale=0.0625)

        def fetch_b(t):
            nc.vector.tensor_scalar(b_win[t][:, :S], banks[T + t][:], 0.0625, None, ALU.mult)

        def per_chunk(name):
            return [tile(f"{name}{c}", [P, T * w], F32, tag=f"{name}{c % 2}") for c, (j0, w) in enumerate(CHUNKS)]

        mn = per_chunk("mn")
        mx = per_chunk("mx")
        v = per_chunk("v")
        y = per_chunk("y")
        z16 = [tile(f"z16_{u}", [P, T * HALF], BF16) for u in range(2)]

        hi = [tile(f"hi{c}", [P, T * w, 2], F32, tag="hi") for c, (j0, w) in enumerate(CHUNKS)]

        def smallest(c, t0, t1):
            w = CHUNKS[c][1]
            m = members[c][:, t0:t1, :].rearrange("p t (j e) -> p (t j) e", e=4)
            nc.vector.tensor_reduce(mn[c][:, t0 * w : t1 * w], m, AX.X, ALU.min)

        def larger_of_pairs(c, t0, t1):
            w = CHUNKS[c][1]
            m = members[c][:, t0:t1, :].rearrange("p t (j u e) -> p (t j) u e", u=2, e=2)
            nc.vector.tensor_tensor(hi[c][:, t0 * w : t1 * w, :], m[:, :, 0, :], m[:, :, 1, :], ALU.max)

        def largest(c):
            nc.vector.tensor_tensor(mx[c][:], hi[c][:, :, 0], hi[c][:, :, 1], ALU.max)

        def against_own(c):
            j0, w = CHUNKS[c]
            for t in range(T):
                rows_t = slice(t * w, (t + 1) * w)
                nc.vector.scalar_tensor_tensor(
                    v[c][:, rows_t], mn[c][:, rows_t], 2.0, banks[t][:, j0 : j0 + w], ALU.mult, ALU.max
                )

        def mix(c, eng):
            eng.tensor_tensor(y[c][:], v[c][:], mx[c][:], ALU.subtract)

        def z16_part(c):
            j0, w = CHUNKS[c]
            at = T * (j0 % HALF)
            return z16[j0 // HALF][:, at : at + T * w]

        def round_z_aside(c):
            w = CHUNKS[c][1]
            nc.gpsimd.tensor_tensor(
                z16_part(c).rearrange("p (j t) -> p j t", t=T),
                y[c][:].rearrange("p (t j) -> p j t", t=T),
                g_n16[:].unsqueeze(1).to_broadcast([P, w, T]),
                ALU.mult,
            )

        def quantise_z(u):
            cols = slice(u * HALF, (u + 1) * HALF)
            nc.vector.quantize_mx(out=z_codes[:, cols].bitcast(FP8X4), scales=z_sc[:, cols], in_=z16[u][:])

        st_win = [tile(f"st_win{t}", [P, S], F32) for t in range(T)]

        def step(t):
            nc.scalar.activation(b_at[t][:], b_win[t][:].indirect(l_n2[:]), ACT.Copy)
            nc.vector.tensor_tensor(st_win[t][:], b_win[t][:, :S], b_at[t][:], ALU.subtract)

        last = NCH - 1
        for c in range(NCH):
            if c in (1, 2):
                fetch_b(c + 1)
            smallest(c, 0, 2)
            if c == 0:
                larger_of_pairs(c, 0, 2)
                fetch_b(1)
            smallest(c, 2, T)
            if c == 0:
                larger_of_pairs(c, 2, T)
                against_own(c)
            else:
                against_own(c)
                larger_of_pairs(c, 0, T)
            if c == 1:
                w_sc = tile("w_sc", [P, 2 * S], U8, tag="members0")
                nc.vector.tensor_copy(
                    w_sc[:].rearrange("p (i t m) -> p i t m", i=2, t=T),
                    w_sc_raw[:].rearrange("p (i m t) -> p i t m", i=2, t=T),
                )
            if c == 2:
                quantise_z(0)
            if c == last:
                step(0)
            largest(c)
            if c < last:
                mix(c, nc.gpsimd)
                round_z_aside(c)
        step(1)
        mix(last, nc.vector)
        step(2)
        scale_round(z16_part(last), y[last][:].rearrange("p (t j) -> p t j", t=T), g_n16[:], CHUNKS[last][1])
        step(3)
        quantise_z(1)

        h_win = [tile(f"h_win{t}", [P, 2 * S], F32) for t in range(T)]
        for pair in range(2):
            for u, t in ((0, 2 * pair), (0, 2 * pair + 1), (1, 2 * pair), (1, 2 * pair + 1)):
                nc.scalar.activation(
                    h_win[t][:, S + u * HALF : S + (u + 1) * HALF],
                    st_win[t][:].indirect(l_n3[:, u * 16 : (u + 1) * 16]),
                    ACT.Copy,
                )
        top = [tile(f"top{u}", [P, T, HALF], F32) for u in range(2)]
        z2_16 = [tile(f"z2_16_{u}", [P, T * HALF], BF16) for u in range(2)]

        def larger(t, u):
            cols = slice(u * HALF, (u + 1) * HALF)
            nc.vector.tensor_tensor(top[u][:, t, :], st_win[t][:, cols], h_win[t][:, S + u * HALF : S + (u + 1) * HALF], ALU.max)

        def h_pass(i, u):
            codes, scales = ((z_codes, z_sc), (z2_codes, z2_sc))[i]
            cols = slice(u * HALF, (u + 1) * HALF)
            for t in (1, 0, 3, 2):
                nc.tensor.matmul_mx(
                    out=banks[T * u + t][:, :HALF],
                    lhsT=w_dealt[i][:, 2 * t * P : 2 * (t + 1) * P].bitcast(FP4X4),
                    lhsT_scale=w_sc[:, i * S + t * P : i * S + (t + 1) * P],
                    rhs=codes[:, cols].bitcast(FP8X4),
                    rhs_scale=scales[:, cols],
                    start=(i == 0),
                    stop=(i == 1),
                )

        def quantise_z2(u):
            cols = slice(u * HALF, (u + 1) * HALF)
            nc.vector.quantize_mx(out=z2_codes[:, cols].bitcast(FP8X4), scales=z2_sc[:, cols], in_=z2_16[u][:])

        def fetch_h(u, t):
            nc.scalar.copy(h_win[t][:, u * HALF : (u + 1) * HALF], banks[T * u + t][:, :HALF])

        h_pass(0, 0)
        h_pass(0, 1)
        for t, u in ((0, 0), (1, 0), (0, 1), (1, 1), (2, 0), (3, 0), (2, 1)):
            larger(t, u)
        scale_round(z2_16[0][:], top[0][:], g_m, HALF)
        larger(3, 1)
        quantise_z2(0)
        h_pass(1, 0)
        for t in range(T):
            fetch_h(0, t)
        scale_round(z2_16[1][:], top[1][:], g_m, HALF)
        quantise_z2(1)
        h_pass(1, 1)

        st2_win = [tile(f"st2_win{t}", [P, 2 * S if t < 2 else S], F32) for t in range(T)]
        h_at_own = [tile(f"h_at{t}", [P, S], F32) for t in (2, 3)]
        h_at = [st2_win[0][:, S:], st2_win[1][:, S:], h_at_own[0][:], h_at_own[1][:]]
        for pair in range(2):
            even, odd = 2 * pair, 2 * pair + 1
            fetch_h(1, odd)
            fetch_h(1, even)
            nc.vector.tensor_copy(h_at[odd], h_win[odd][:].indirect(l_n4[:]))
            nc.scalar.activation(h_at[even], h_win[even][:].indirect(l_n4[:]), ACT.Copy)
            for s in (even, odd):
                nc.vector.tensor_tensor(st2_win[s][:, :S], h_win[s][:, :S], h_at[s], ALU.subtract)

        gate = [tile(f"gate{t}", [P, S], F32) for t in range(T)]
        res = tile("res", [P, T, S], F32)
        r16 = tile("r16", [P, T * S], BF16)
        o_codes = tile("o_codes", [P, S], U32)
        o_sc = tile("o_sc", [P, S], U8)
        out_rows = out_0.rearrange("(p t) j -> p t j", t=T)
        out_words = out_1[0].rearrange("p n t -> p (n t)").bitcast(I32)

        def gated(t, j0, w):
            cols = slice(j0, j0 + w)
            nc.scalar.activation(
                gate[t][:, cols],
                st2_win[t][:].indirect(l_n5[:, j0 // 16 : (j0 + w) // 16]),
                ACT.Sigmoid,
                bias=bias[:, t : t + 1],
                scale=slope[:, t : t + 1],
            )
            nc.vector.tensor_tensor(res[:, t, cols], h_win[t][:, cols], gate[t][:, cols], ALU.mult)

        def round_out(j0, w):
            cols = slice(j0, j0 + w)
            nc.sync.dma_start(out=out_rows[:, 2:4, cols], in_=res[:, 2:4, cols])
            nc.vector.tensor_copy(
                r16[:, T * j0 : T * (j0 + w)].rearrange("p (c i t) -> p c t i", t=T, i=2),
                res[:, :, cols].rearrange("p t (c i) -> p c t i", i=2),
            )

        def quantise_out(j0, w):
            cols = slice(j0, j0 + w)
            nc.vector.quantize_mx(
                out=o_codes[:, cols].bitcast(FP8X4), scales=o_sc[:, cols], in_=r16[:, T * j0 : T * (j0 + w)]
            )
            nc.sync.dma_start(out=out_words[:, cols], in_=o_codes[:, cols].bitcast(I32))

        for t in (0, 1):
            gated(t, 0, S)
        nc.sync.dma_start(out=out_rows[:, 0:2, :], in_=res[:, 0:2, :])
        pieces = ((0, 256), (256, 128), (384, 128))
        gated(2, *pieces[0])
        gated(3, *pieces[0])
        for k in range(1, len(pieces)):
            gated(2, *pieces[k])
            round_out(*pieces[k - 1])
            gated(3, *pieces[k])
            quantise_out(*pieces[k - 1])
        round_out(*pieces[-1])
        quantise_out(*pieces[-1])
        for q in range(4):
            nc.scalar.dma_start(
                out=out_2[0, 4 * q : 4 * q + 4, :].bitcast(I32), in_=o_sc[32 * q : 32 * q + 4, :].bitcast(I32)
            )
